import numpy as np
import ml_dtypes


def mxq(x, axis, fmt="e4m3"):
    dtype, down = {"e4m3": (ml_dtypes.float8_e4m3fn, 7), "e5m2": (ml_dtypes.float8_e5m2, 14)}[fmt]
    v = np.moveaxis(np.asarray(x, np.float32).astype(ml_dtypes.bfloat16).astype(np.float64), axis, -1)
    blocks = v.reshape(v.shape[:-1] + (-1, 32))
    amax = np.abs(blocks).max(-1, keepdims=True)
    byte = np.maximum(np.where(amax > 0, np.frexp(amax)[1] - 1 + 127, 0) - down, 1)
    scale = np.exp2(byte - 127.0)
    codes = (blocks / scale).astype(np.float32).astype(dtype).astype(np.float64)
    return np.moveaxis((codes * scale).reshape(v.shape), -1, axis)


WIDE = False


def mx_kscale(k):
    if not WIDE:
        return np.ones(k)
    levels = np.array([10, -10, 5, -5, 0])
    if k % 512:
        return np.exp2(np.random.permutation(np.resize(levels, k // 32))).repeat(32)
    a = np.empty((k // 512, 16))
    for p in range(k // 512):
        a[p, :8] = np.random.permutation(np.resize(levels, 8))
        for g in range(8):
            far = levels[np.abs(levels - a[p, g]) >= 10]
            a[p, g + 8] = far[np.random.randint(len(far))]
    return np.exp2(a.ravel()).repeat(32)


def f64(x):
    return np.asarray(x).astype(np.float64)


def striped(idx):
    return np.tile(idx.reshape(-1, 16).T, (8, 1)).astype(np.uint16)


def unstriped(offs):
    return offs[:16].T.reshape(-1).astype(np.int64)


def pack_weight(w):
    k, n = w.shape
    w = f64(np.asarray(w, np.float32).astype(ml_dtypes.bfloat16)).reshape(k // 32, 32, n)
    amax = np.abs(w).max(1)
    byte = np.clip(np.where(amax > 0, np.frexp(amax)[1] - 1 + 127 - 7, 1), 1, 254)
    scaled = (w * np.exp2(127.0 - byte)[:, None, :]).reshape(k, n).astype(np.float32)
    words = np.ascontiguousarray(scaled.reshape(k // 512, 128, 4, n).transpose(0, 1, 3, 2)).astype(ml_dtypes.float8_e4m3fn).view(np.uint8)
    return words, np.ascontiguousarray(byte.astype(np.uint8).reshape(k // 512, 16, n))


def unpack_weight(words, scales):
    g, p, n, _ = words.shape
    vals = np.ascontiguousarray(words).view(ml_dtypes.float8_e4m3fn).astype(np.float64) * np.repeat(np.exp2(scales.astype(np.float64) - 127.0), 8, axis=1)[..., None]
    return vals.transpose(0, 1, 3, 2).reshape(g * 512, n)


def silu(v):
    return v / (1.0 + np.exp(-np.maximum(v, -700.0)))

def planes(y):
    n, m = y.shape
    v = y.astype(np.float32).astype(ml_dtypes.bfloat16).astype(np.float64).reshape(n // 32, 32, m)
    top = np.abs(v).max(1)
    byte = np.clip(np.where(top > 0, np.frexp(top)[1] - 1 + 127 - 7, 1), 1, 254)
    codes = (v * np.exp2(127.0 - byte)[:, None, :]).reshape(n, m).astype(np.float32).astype(ml_dtypes.float8_e4m3fn).view(np.uint8)
    words = codes.reshape(n // 512, 128, 4, m).transpose(0, 1, 3, 2)
    return np.ascontiguousarray(words), np.ascontiguousarray(byte.astype(np.uint8).reshape(n // 512, 16, m))


K, T, H, J, U = 1024, 512, 512, 512, 1024


def setup_inputs():
    n = np.random.standard_normal
    s = mx_kscale(K)[:, None]
    u = mx_kscale(H)
    r = mx_kscale(J)[:, None]
    packed_xT = pack_weight(n((K, T)) * s)
    packed_w2 = pack_weight(n((H, H)) / np.sqrt(2 * H) / u[:, None])
    return {
        "x_words": packed_xT[0],
        "x_scales": packed_xT[1],
        "aT": (n((J, U)) * r).astype(np.float32),
        "w1": (n((K, H)) / np.sqrt(K) / s * u).astype(np.float32),
        "w3": (n((J, H)) / np.sqrt(J) / r).astype(np.float32),
        "w2_words": packed_w2[0],
        "w2_scales": packed_w2[1],
        "pos1": striped(np.random.permutation(T)),
        "pos2": striped(np.random.permutation(T)),
    }


def reference(x_words, x_scales, aT, w1, w3, w2_words, w2_scales, pos1, pos2):
    xq = unpack_weight(x_words, x_scales)
    h = silu(mxq(f64(w1), 0, "e4m3").T @ xq)
    f = mxq(f64(w3), 0, "e4m3").T @ mxq(f64(aT), 0, "e4m3")
    z = h[:, unstriped(pos1)] * f[:, :T] + h[:, unstriped(pos2)] * f[:, T:2 * T]
    out_0 = silu(unpack_weight(w2_words, w2_scales).T @ mxq(z, 0, "e4m3"))
    return (out_0,) + planes(out_0)

@@ -1,0 +1,222 @@
+from contextlib import ExitStack
+
+import concourse.mybir as mybir
+
+K, T, H, J, U = 1024, 512, 512, 512, 1024
+FLOPS = 2 * (K * H * T + J * H * U + H * H * T)
+
+F32 = mybir.dt.float32
+BF16 = mybir.dt.bfloat16
+I32 = mybir.dt.int32
+U32 = mybir.dt.uint32
+U16 = mybir.dt.uint16
+U8 = mybir.dt.uint8
+FP8X4 = mybir.dt.float8_e4m3fn_x4
+SILU = mybir.ActivationFunctionType.Silu
+MULT = mybir.AluOpType.mult
+ADD = mybir.AluOpType.add
+
+P = 128
+PACK = 4
+K_PASS = P * PACK
+QUADS = 4
+HALF = 256
+BLOCK = 128
+VECTOR_COLS = 352
+
+
+def tile_picked_wdime_silu_lo_kernel(
+    tc, x_words, x_scales, aT, w1, w3, w2_words, w2_scales, pos1, pos2, out_0, out_1, out_2
+):
+    nc = tc.nc
+    passes = K // K_PASS
+
+    with ExitStack() as ctx:
+        keep = ctx.enter_context(tc.tile_pool(name="keep", bufs=1))
+        psum = ctx.enter_context(tc.psum_pool(name="psum", bufs=4))
+
+        def sbuf(name, shape, dtype):
+            return keep.tile(shape, dtype, name=name, align_bytes=64)
+
+        def load_rows(name, rows):
+            raw = sbuf(name, [P, PACK, rows.shape[1]], F32)
+            nc.sync.dma_start(out=raw[:], in_=rows.rearrange("(p j) c -> p j c", j=PACK))
+            return raw
+
+        def load_words(name, words):
+            tile = sbuf(name, [P, words.shape[1]], U32)
+            nc.sync.dma_start(out=tile[:].bitcast(I32), in_=words.rearrange("p n t -> p (n t)").bitcast(I32))
+            return tile
+
+        def load_scales(plane, scales):
+            for q in range(QUADS):
+                nc.sync.dma_start(
+                    out=plane[32 * q : 32 * q + 4].bitcast(I32),
+                    in_=scales[:, 4 * q : 4 * q + 4, :].rearrange("g r c -> r g c").bitcast(I32),
+                )
+
+        def load_list(name, pos):
+            offsets = keep.tile([P, T // 16], U16, name=name)
+            nc.sync.dma_start(offsets[:], pos)
+            return offsets
+
+        def copy_on(engine, out, in_):
+            if engine == "vector":
+                nc.vector.tensor_copy(out=out, in_=in_)
+            else:
+                nc.scalar.copy(out=out, in_=in_)
+
+        def round_weights(name, raw):
+            grouped = sbuf(name, [P, PACK, P, PACK], BF16)
+            dst = grouped[:].rearrange("p t m j -> p m j t")
+            src = raw[:].rearrange("p j (m t) -> p m j t", t=PACK)
+            cut = VECTOR_COLS // PACK
+            copy_on("vector", dst[:, :cut], src[:, :cut])
+            copy_on("scalar", dst[:, cut:], src[:, cut:])
+            return grouped[:].rearrange("p t m j -> p (t m j)")
+
+        def round_columns(name, raw, vector_cols):
+            width = raw.shape[2]
+            grouped = sbuf(name, [P, width, PACK], BF16)
+            dst = grouped[:].rearrange("p (c i) j -> p c j i", i=2)
+            src = raw[:].rearrange("p j (c i) -> p c j i", i=2)
+            cut = vector_cols // 2
+            if cut:
+                copy_on("vector", dst[:, :cut], src[:, :cut])
+            copy_on("scalar", dst[:, cut:], src[:, cut:])
+            return grouped[:].rearrange("p c j -> p (c j)")
+
+        def quantize(name, grouped, calls):
+            width = grouped.shape[1] // PACK
+            codes = sbuf(name + "_codes", [P, width], U32)
+            scales = sbuf(name + "_scales", [P, width], U8)
+            step = width // calls
+            for c0 in range(0, width, step):
+                nc.vector.quantize_mx(
+                    out=codes[:, c0 : c0 + step].bitcast(FP8X4),
+                    scales=scales[:, c0 : c0 + step],
+                    in_=grouped[:, PACK * c0 : PACK * (c0 + step)],
+                )
+            return codes, scales
+
+        def matmul(out, weights, t, codes, scales, start=True, stop=True):
+            cols = slice(P * t, P * (t + 1))
+            nc.tensor.matmul_mx(
+                out=out,
+                lhsT=weights[0][:, cols].bitcast(FP8X4),
+                lhsT_scale=weights[1][:, cols],
+                rhs=codes.bitcast(FP8X4),
+                rhs_scale=scales,
+                start=start,
+                stop=stop,
+            )
+
+        x_plane = sbuf("x_plane", [P, passes, T], U8)
+        w2_plane_raw = sbuf("w2_plane_raw", [P, 1, H], U8)
+        nc.vector.memset(x_plane[:].bitcast(I32), 0)
+        nc.vector.memset(w2_plane_raw[:].bitcast(I32), 0)
+
+        w3_raw = load_rows("w3_raw", w3)
+        a0_raw = load_rows("a0_raw", aT[:, :T])
+        w1_raw = [load_rows("w1_raw0", w1[:K_PASS, :])]
+        load_scales(x_plane, x_scales)
+        offsets = [load_list("offsets1", pos1), load_list("offsets2", pos2)]
+        w1_raw.append(load_rows("w1_raw1", w1[K_PASS:, :]))
+        load_scales(w2_plane_raw, w2_scales)
+        x_codes = [load_words("x_codes%d" % g, x_words[g]) for g in range(passes)]
+        w2_raw = load_words("w2_raw", w2_words[0])
+        a1_raw = [load_rows("a1_raw%d" % s, aT[:, T + HALF * s : T + HALF * (s + 1)]) for s in range(T // HALF)]
+
+        w3_q = quantize("w3", round_weights("w3_bf", w3_raw), 1)
+        a0_codes, a0_scales = quantize("a0", round_columns("a0_bf", a0_raw, VECTOR_COLS), 1)
+        f0 = []
+        for t in range(PACK):
+            bank = psum.tile([P, T], F32, name="f_bank", tag="f_bank")
+            matmul(bank[:], w3_q, t, a0_codes[:], a0_scales[:])
+            f0.append(sbuf("f0_%d" % t, [P, T], F32))
+            nc.scalar.copy(out=f0[t][:], in_=bank[:])
+
+        w1_q = [quantize("w1_%d" % g, round_weights("w1_bf%d" % g, w1_raw[g]), 1 + 3 * g) for g in range(passes)]
+
+        w2_plane = sbuf("w2_plane", [P, H], U8)
+        nc.vector.tensor_copy(
+            out=w2_plane[:].rearrange("p (t m) -> p m t", t=PACK),
+            in_=w2_plane_raw[:, 0, :].rearrange("p (m t) -> p m t", t=PACK),
+        )
+
+        h = []
+        for t in range(PACK):
+            bank = psum.tile([P, T], F32, name="h_bank", tag="acc_bank")
+            for g in range(passes):
+                matmul(bank[:], w1_q[g], t, x_codes[g][:], x_plane[:, g, :], start=(g == 0), stop=(g == passes - 1))
+            h.append(sbuf("h_%d" % t, [P, T], F32))
+            nc.scalar.activation(out=h[t][:], in_=bank[:], func=SILU)
+
+        w2_codes = sbuf("w2_codes", [P, H], U32)
+        nc.vector.tensor_copy(
+            out=w2_codes[:].bitcast(I32).rearrange("p (t m) -> p m t", t=PACK),
+            in_=w2_raw[:].bitcast(I32).rearrange("p (m t) -> p m t", t=PACK),
+        )
+        w2_q = (w2_codes, w2_plane)
+
+        f1 = []
+        for s in range(T // HALF):
+            codes, scales = quantize("a1_%d" % s, round_columns("a1_bf%d" % s, a1_raw[s], 0), 1)
+            pairs = []
+            for u in range(PACK // 2):
+                bank = psum.tile([P, 2, HALF], F32, name="f_bank", tag="f_bank")
+                for e in range(2):
+                    matmul(bank[:, e, :], w3_q, 2 * u + e, codes[:], scales[:])
+                pairs.append(sbuf("f1_%d_%d" % (s, u), [P, 2, HALF], F32))
+                nc.scalar.copy(out=pairs[u][:], in_=bank[:])
+            f1.append(pairs)
+
+        def gather(out, t, d, v0, width, factor):
+            picks = offsets[d][:, v0 // 16 : (v0 + width) // 16]
+            nc.vector.tensor_tensor(out, h[t][:].indirect(picks), factor, MULT)
+
+        first = sbuf("first", [P, PACK, T], F32)
+        for t in range(PACK):
+            for v0 in range(0, T, HALF):
+                gather(first[:, t, v0 : v0 + HALF], t, 0, v0, HALF, f0[t][:, v0 : v0 + HALF])
+
+        out_codes = sbuf("out_codes", [P, T], U32)
+        out_scales = sbuf("out_scales", [P, T], U8)
+        out_rows = out_0.rearrange("(p t) v -> p t v", t=PACK)
+        out_words = out_1[0].rearrange("p n t -> p (n t)").bitcast(I32)
+        for b in range(T // BLOCK):
+            v0 = BLOCK * b
+            cols = slice(v0, v0 + BLOCK)
+            s, c0 = divmod(v0, HALF)
+            second = sbuf("second%d" % b, [P, PACK, BLOCK], F32)
+            for t in range(PACK):
+                gather(second[:, t, :], t, 1, v0, BLOCK, f1[s][t // 2][:, t % 2, c0 : c0 + BLOCK])
+            z = sbuf("z%d" % b, [P, BLOCK, PACK], BF16)
+            nc.vector.tensor_tensor(
+                z[:].rearrange("p (c i) t -> p c t i", i=2),
+                first[:, :, cols].rearrange("p t (c i) -> p c t i", i=2),
+                second[:].rearrange("p t (c i) -> p c t i", i=2),
+                ADD,
+            )
+            z_codes, z_scales = quantize("z%d" % b, z[:].rearrange("p c t -> p (c t)"), 1)
+            bank = psum.tile([P, PACK, BLOCK], F32, name="out_bank", tag="acc_bank")
+            for t in range(PACK):
+                matmul(bank[:, t, :], w2_q, t, z_codes[:], z_scales[:])
+            y_bf = sbuf("y_bf%d" % b, [P, BLOCK, PACK], BF16)
+            nc.scalar.activation(out=y_bf[:], in_=bank[:].rearrange("p t c -> p c t"), func=SILU)
+            y = sbuf("y%d" % b, [P, PACK, BLOCK], F32)
+            nc.scalar.activation(out=y[:], in_=bank[:], func=SILU)
+            nc.vector.quantize_mx(
+                out=out_codes[:, cols].bitcast(FP8X4),
+                scales=out_scales[:, cols],
+                in_=y_bf[:].rearrange("p c t -> p (c t)"),
+            )
+            nc.sync.dma_start(out=out_rows[:, :, cols], in_=y[:])
+            nc.sync.dma_start(out=out_words[:, cols], in_=out_codes[:, cols].bitcast(I32))
+
+        for q in range(QUADS):
+            queue = nc.sync if q < 2 else nc.scalar
+            queue.dma_start(
+                out=out_2[0][4 * q : 4 * q + 4, :].bitcast(I32),
+                in_=out_scales[32 * q : 32 * q + 4, :].bitcast(I32),
+            )

@@ -23,6 +23,8 @@ QUADS = 4
 HALF = 256
 BLOCK = 128
 VECTOR_COLS = 352
+FIRST_CUT = 384
+BLOCKS = ((0, 256), (256, 128), (384, 128))
 
 
 def tile_picked_wdime_silu_lo_kernel(
@@ -35,8 +37,8 @@ def tile_picked_wdime_silu_lo_kernel(
         keep = ctx.enter_context(tc.tile_pool(name="keep", bufs=1))
         psum = ctx.enter_context(tc.psum_pool(name="psum", bufs=4))
 
-        def sbuf(name, shape, dtype):
-            return keep.tile(shape, dtype, name=name, align_bytes=64)
+        def sbuf(name, shape, dtype, tag=None):
+            return keep.tile(shape, dtype, name=name, tag=tag or name, align_bytes=64)
 
         def load_rows(name, rows):
             raw = sbuf(name, [P, PACK, rows.shape[1]], F32)
@@ -50,7 +52,7 @@ def tile_picked_wdime_silu_lo_kernel(
 
         def load_scales(plane, scales):
             for q in range(QUADS):
-                nc.sync.dma_start(
+                nc.gpsimd.dma_start(
                     out=plane[32 * q : 32 * q + 4].bitcast(I32),
                     in_=scales[:, 4 * q : 4 * q + 4, :].rearrange("g r c -> r g c").bitcast(I32),
                 )
@@ -66,20 +68,21 @@ def tile_picked_wdime_silu_lo_kernel(
             else:
                 nc.scalar.copy(out=out, in_=in_)
 
-        def round_weights(name, raw):
+        def round_weights(name, raw, vector_cols):
             grouped = sbuf(name, [P, PACK, P, PACK], BF16)
             dst = grouped[:].rearrange("p t m j -> p m j t")
             src = raw[:].rearrange("p j (m t) -> p m j t", t=PACK)
-            cut = VECTOR_COLS // PACK
+            cut = vector_cols // PACK
             copy_on("vector", dst[:, :cut], src[:, :cut])
-            copy_on("scalar", dst[:, cut:], src[:, cut:])
+            if cut < P:
+                copy_on("scalar", dst[:, cut:], src[:, cut:])
             return grouped[:].rearrange("p t m j -> p (t m j)")
 
         def round_columns(name, raw, vector_cols):
             width = raw.shape[2]
             grouped = sbuf(name, [P, width, PACK], BF16)
             dst = grouped[:].rearrange("p (c i) j -> p c j i", i=2)
-            src = raw[:].rearrange("p j (c i) -> p c j i", i=2)
+            src = raw.rearrange("p j (c i) -> p c j i", i=2)
             cut = vector_cols // 2
             if cut:
                 copy_on("vector", dst[:, :cut], src[:, :cut])
@@ -111,24 +114,32 @@ def tile_picked_wdime_silu_lo_kernel(
                 stop=stop,
             )
 
+        warm = sbuf("warm", [P, 2], F32)
+        nc.vector.memset(warm[:, 0:1], 0.0)
+        nc.scalar.activation(out=warm[:, 1:2], in_=warm[:, 0:1], func=SILU)
+
         x_plane = sbuf("x_plane", [P, passes, T], U8)
         w2_plane_raw = sbuf("w2_plane_raw", [P, 1, H], U8)
-        nc.vector.memset(x_plane[:].bitcast(I32), 0)
-        nc.vector.memset(w2_plane_raw[:].bitcast(I32), 0)
+        nc.gpsimd.memset(x_plane[:].bitcast(I32), 0)
+        load_scales(x_plane, x_scales)
+        nc.gpsimd.memset(w2_plane_raw[:].bitcast(I32), 0)
+        load_scales(w2_plane_raw, w2_scales)
 
         w3_raw = load_rows("w3_raw", w3)
         a0_raw = load_rows("a0_raw", aT[:, :T])
         w1_raw = [load_rows("w1_raw0", w1[:K_PASS, :])]
-        load_scales(x_plane, x_scales)
         offsets = [load_list("offsets1", pos1), load_list("offsets2", pos2)]
         w1_raw.append(load_rows("w1_raw1", w1[K_PASS:, :]))
-        load_scales(w2_plane_raw, w2_scales)
         x_codes = [load_words("x_codes%d" % g, x_words[g]) for g in range(passes)]
         w2_raw = load_words("w2_raw", w2_words[0])
         a1_raw = [load_rows("a1_raw%d" % s, aT[:, T + HALF * s : T + HALF * (s + 1)]) for s in range(T // HALF)]
 
-        w3_q = quantize("w3", round_weights("w3_bf", w3_raw), 1)
-        a0_codes, a0_scales = quantize("a0", round_columns("a0_bf", a0_raw, VECTOR_COLS), 1)
+        w3_q = quantize("w3", round_weights("w3_bf", w3_raw, VECTOR_COLS), 1)
+        a0_codes, a0_scales = quantize("a0", round_columns("a0_bf", a0_raw[:], VECTOR_COLS), 1)
+        w1_q = [
+            quantize("w1_0", round_weights("w1_bf0", w1_raw[0], H), 1),
+            quantize("w1_1", round_weights("w1_bf1", w1_raw[1], 384), PACK),
+        ]
         f0 = []
         for t in range(PACK):
             bank = psum.tile([P, T], F32, name="f_bank", tag="f_bank")
@@ -136,9 +147,8 @@ def tile_picked_wdime_silu_lo_kernel(
             f0.append(sbuf("f0_%d" % t, [P, T], F32))
             nc.scalar.copy(out=f0[t][:], in_=bank[:])
 
-        w1_q = [quantize("w1_%d" % g, round_weights("w1_bf%d" % g, w1_raw[g]), 1 + 3 * g) for g in range(passes)]
 
-        w2_plane = sbuf("w2_plane", [P, H], U8)
+        w2_plane = sbuf("w2_plane", [P, H], U8, tag="w1_raw1")
         nc.vector.tensor_copy(
             out=w2_plane[:].rearrange("p (t m) -> p m t", t=PACK),
             in_=w2_plane_raw[:, 0, :].rearrange("p (m t) -> p m t", t=PACK),
@@ -152,7 +162,7 @@ def tile_picked_wdime_silu_lo_kernel(
             h.append(sbuf("h_%d" % t, [P, T], F32))
             nc.scalar.activation(out=h[t][:], in_=bank[:], func=SILU)
 
-        w2_codes = sbuf("w2_codes", [P, H], U32)
+        w2_codes = sbuf("w2_codes", [P, H], U32, tag="w1_bf1")
         nc.vector.tensor_copy(
             out=w2_codes[:].bitcast(I32).rearrange("p (t m) -> p m t", t=PACK),
             in_=w2_raw[:].bitcast(I32).rearrange("p (m t) -> p m t", t=PACK),
@@ -161,7 +171,7 @@ def tile_picked_wdime_silu_lo_kernel(
 
         f1 = []
         for s in range(T // HALF):
-            codes, scales = quantize("a1_%d" % s, round_columns("a1_bf%d" % s, a1_raw[s], 0), 1)
+            codes, scales = quantize("a1_%d" % s, round_columns("a1_bf%d" % s, a1_raw[s][:], 0), 1)
             pairs = []
             for u in range(PACK // 2):
                 bank = psum.tile([P, 2, HALF], F32, name="f_bank", tag="f_bank")
@@ -175,37 +185,45 @@ def tile_picked_wdime_silu_lo_kernel(
             picks = offsets[d][:, v0 // 16 : (v0 + width) // 16]
             nc.vector.tensor_tensor(out, h[t][:].indirect(picks), factor, MULT)
 
-        first = sbuf("first", [P, PACK, T], F32)
-        for t in range(PACK):
-            for v0 in range(0, T, HALF):
-                gather(first[:, t, v0 : v0 + HALF], t, 0, v0, HALF, f0[t][:, v0 : v0 + HALF])
+        first = []
+        for v0, width, tag in ((0, FIRST_CUT, None), (FIRST_CUT, T - FIRST_CUT, "a1_bf0")):
+            tile = sbuf("first%d" % v0, [P, PACK, width], F32, tag=tag)
+            for t in range(PACK):
+                gather(tile[:, t, :], t, 0, v0, width, f0[t][:, v0 : v0 + width])
+            first.append(tile)
 
+        ring = sbuf("ring", [P, PACK + 1, HALF], F32, tag="a1_bf1")
         out_codes = sbuf("out_codes", [P, T], U32)
         out_scales = sbuf("out_scales", [P, T], U8)
         out_rows = out_0.rearrange("(p t) v -> p t v", t=PACK)
         out_words = out_1[0].rearrange("p n t -> p (n t)").bitcast(I32)
-        for b in range(T // BLOCK):
-            v0 = BLOCK * b
-            cols = slice(v0, v0 + BLOCK)
+        for b, (v0, width) in enumerate(BLOCKS):
+            cols = slice(v0, v0 + width)
             s, c0 = divmod(v0, HALF)
-            second = sbuf("second%d" % b, [P, PACK, BLOCK], F32)
-            for t in range(PACK):
-                gather(second[:, t, :], t, 1, v0, BLOCK, f1[s][t // 2][:, t % 2, c0 : c0 + BLOCK])
-            z = sbuf("z%d" % b, [P, BLOCK, PACK], BF16)
+            second = ring[:, b % 2 : b % 2 + PACK, :width]
+            for t in range(PACK) if b % 2 == 0 else (PACK - 1, *range(PACK - 1)):
+                gather(second[:, t, :], t, 1, v0, width, f1[s][t // 2][:, t % 2, c0 : c0 + width])
+            if v0 < FIRST_CUT:
+                addend = first[0][:, :, cols]
+            else:
+                addend = first[1][:, :, v0 - FIRST_CUT : v0 - FIRST_CUT + width]
+            z = sbuf("z%d" % b, [P, width, PACK], BF16)
             nc.vector.tensor_tensor(
                 z[:].rearrange("p (c i) t -> p c t i", i=2),
-                first[:, :, cols].rearrange("p t (c i) -> p c t i", i=2),
-                second[:].rearrange("p t (c i) -> p c t i", i=2),
+                addend.rearrange("p t (c i) -> p c t i", i=2),
+                second.rearrange("p t (c i) -> p c t i", i=2),
                 ADD,
             )
             z_codes, z_scales = quantize("z%d" % b, z[:].rearrange("p c t -> p (c t)"), 1)
-            bank = psum.tile([P, PACK, BLOCK], F32, name="out_bank", tag="acc_bank")
-            for t in range(PACK):
-                matmul(bank[:, t, :], w2_q, t, z_codes[:], z_scales[:])
-            y_bf = sbuf("y_bf%d" % b, [P, BLOCK, PACK], BF16)
-            nc.scalar.activation(out=y_bf[:], in_=bank[:].rearrange("p t c -> p c t"), func=SILU)
-            y = sbuf("y%d" % b, [P, PACK, BLOCK], F32)
-            nc.scalar.activation(out=y[:], in_=bank[:], func=SILU)
+            y_bf = sbuf("y_bf%d" % b, [P, width, PACK], BF16)
+            y = sbuf("y%d" % b, [P, PACK, width], F32)
+            for u0 in range(0, width, BLOCK):
+                part = slice(u0, u0 + BLOCK)
+                bank = psum.tile([P, PACK, BLOCK], F32, name="out_bank", tag="acc_bank")
+                for t in range(PACK):
+                    matmul(bank[:, t, :], w2_q, t, z_codes[:, part], z_scales[:, part])
+                nc.scalar.activation(out=y_bf[:, part, :], in_=bank[:].rearrange("p t c -> p c t"), func=SILU)
+                nc.scalar.activation(out=y[:, :, part], in_=bank[:], func=SILU)
             nc.vector.quantize_mx(
                 out=out_codes[:, cols].bitcast(FP8X4),
                 scales=out_scales[:, cols],

@@ -24,7 +24,7 @@ HALF = 256
 BLOCK = 128
 VECTOR_COLS = 352
 FIRST_CUT = 384
-BLOCKS = ((0, 256), (256, 128), (384, 128))
+BLOCKS = ((0, (256,)), (256, (128,)), (384, (128,)))
 
 
 def tile_picked_wdime_silu_lo_kernel(
@@ -50,9 +50,9 @@ def tile_picked_wdime_silu_lo_kernel(
             nc.sync.dma_start(out=tile[:].bitcast(I32), in_=words.rearrange("p n t -> p (n t)").bitcast(I32))
             return tile
 
-        def load_scales(plane, scales):
+        def load_scales(queue, plane, scales):
             for q in range(QUADS):
-                nc.gpsimd.dma_start(
+                queue.dma_start(
                     out=plane[32 * q : 32 * q + 4].bitcast(I32),
                     in_=scales[:, 4 * q : 4 * q + 4, :].rearrange("g r c -> r g c").bitcast(I32),
                 )
@@ -68,15 +68,20 @@ def tile_picked_wdime_silu_lo_kernel(
             else:
                 nc.scalar.copy(out=out, in_=in_)
 
-        def round_weights(name, raw, vector_cols):
-            grouped = sbuf(name, [P, PACK, P, PACK], BF16)
-            dst = grouped[:].rearrange("p t m j -> p m j t")
-            src = raw[:].rearrange("p j (m t) -> p m j t", t=PACK)
-            cut = vector_cols // PACK
-            copy_on("vector", dst[:, :cut], src[:, :cut])
-            if cut < P:
-                copy_on("scalar", dst[:, cut:], src[:, cut:])
-            return grouped[:].rearrange("p t m j -> p (t m j)")
+        def quantize_weights(name, raw, engines):
+            codes = sbuf(name + "_codes", [P, H], U32)
+            scales = sbuf(name + "_scales", [P, H], U8)
+            src = raw[:].rearrange("p j (m u e) -> p u m j e", u=2, e=2)
+            for u, engine in enumerate(engines):
+                grouped = sbuf("%s_bf%d" % (name, u), [P, 2, P, PACK], BF16)
+                copy_on(engine, grouped[:].rearrange("p e m j -> p m j e"), src[:, u])
+                cols = slice(2 * P * u, 2 * P * (u + 1))
+                nc.vector.quantize_mx(
+                    out=codes[:, cols].bitcast(FP8X4),
+                    scales=scales[:, cols],
+                    in_=grouped[:].rearrange("p e m j -> p (e m j)"),
+                )
+            return codes, scales
 
         def round_columns(name, raw, vector_cols):
             width = raw.shape[2]
@@ -102,6 +107,16 @@ def tile_picked_wdime_silu_lo_kernel(
                 )
             return codes, scales
 
+        def quantize_pieces(codes, scales, grouped, pieces):
+            c0 = 0
+            for n in pieces:
+                nc.vector.quantize_mx(
+                    out=codes[:, c0 : c0 + n].bitcast(FP8X4),
+                    scales=scales[:, c0 : c0 + n],
+                    in_=grouped[:, c0 : c0 + n, :].rearrange("p c t -> p (c t)"),
+                )
+                c0 += n
+
         def matmul(out, weights, t, codes, scales, start=True, stop=True):
             cols = slice(P * t, P * (t + 1))
             nc.tensor.matmul_mx(
@@ -120,25 +135,30 @@ def tile_picked_wdime_silu_lo_kernel(
 
         x_plane = sbuf("x_plane", [P, passes, T], U8)
         w2_plane_raw = sbuf("w2_plane_raw", [P, 1, H], U8)
-        nc.gpsimd.memset(x_plane[:].bitcast(I32), 0)
-        load_scales(x_plane, x_scales)
+        x_rows = sbuf("x_rows", [P, passes, T], U8)
+        nc.vector.memset(x_plane[:].bitcast(I32), 0)
         nc.gpsimd.memset(w2_plane_raw[:].bitcast(I32), 0)
-        load_scales(w2_plane_raw, w2_scales)
+        load_scales(nc.gpsimd, w2_plane_raw, w2_scales)
 
         w3_raw = load_rows("w3_raw", w3)
         a0_raw = load_rows("a0_raw", aT[:, :T])
+        load_scales(nc.sync, x_rows, x_scales)
         w1_raw = [load_rows("w1_raw0", w1[:K_PASS, :])]
-        offsets = [load_list("offsets1", pos1), load_list("offsets2", pos2)]
+        offsets = [load_list("offsets1", pos1)]
         w1_raw.append(load_rows("w1_raw1", w1[K_PASS:, :]))
+        offsets.append(load_list("offsets2", pos2))
         x_codes = [load_words("x_codes%d" % g, x_words[g]) for g in range(passes)]
         w2_raw = load_words("w2_raw", w2_words[0])
         a1_raw = [load_rows("a1_raw%d" % s, aT[:, T + HALF * s : T + HALF * (s + 1)]) for s in range(T // HALF)]
 
-        w3_q = quantize("w3", round_weights("w3_bf", w3_raw, VECTOR_COLS), 1)
+        w3_q = quantize_weights("w3", w3_raw, ("vector", "scalar"))
         a0_codes, a0_scales = quantize("a0", round_columns("a0_bf", a0_raw[:], VECTOR_COLS), 1)
+        for q in range(QUADS):
+            rows = slice(32 * q, 32 * q + 4)
+            nc.vector.tensor_copy(out=x_plane[rows].bitcast(I32), in_=x_rows[rows].bitcast(I32))
         w1_q = [
-            quantize("w1_0", round_weights("w1_bf0", w1_raw[0], H), 1),
-            quantize("w1_1", round_weights("w1_bf1", w1_raw[1], 384), PACK),
+            quantize_weights("w1_0", w1_raw[0], ("vector", "vector")),
+            quantize_weights("w1_1", w1_raw[1], ("vector", "scalar")),
         ]
         f0 = []
         for t in range(PACK):
@@ -148,7 +168,7 @@ def tile_picked_wdime_silu_lo_kernel(
             nc.scalar.copy(out=f0[t][:], in_=bank[:])
 
 
-        w2_plane = sbuf("w2_plane", [P, H], U8, tag="w1_raw1")
+        w2_plane = sbuf("w2_plane", [P, H], U8, tag="w1_1_bf0")
         nc.vector.tensor_copy(
             out=w2_plane[:].rearrange("p (t m) -> p m t", t=PACK),
             in_=w2_plane_raw[:, 0, :].rearrange("p (m t) -> p m t", t=PACK),
@@ -162,7 +182,7 @@ def tile_picked_wdime_silu_lo_kernel(
             h.append(sbuf("h_%d" % t, [P, T], F32))
             nc.scalar.activation(out=h[t][:], in_=bank[:], func=SILU)
 
-        w2_codes = sbuf("w2_codes", [P, H], U32, tag="w1_bf1")
+        w2_codes = sbuf("w2_codes", [P, H], U32, tag="w1_1_bf1")
         nc.vector.tensor_copy(
             out=w2_codes[:].bitcast(I32).rearrange("p (t m) -> p m t", t=PACK),
             in_=w2_raw[:].bitcast(I32).rearrange("p (m t) -> p m t", t=PACK),
@@ -197,7 +217,8 @@ def tile_picked_wdime_silu_lo_kernel(
         out_scales = sbuf("out_scales", [P, T], U8)
         out_rows = out_0.rearrange("(p t) v -> p t v", t=PACK)
         out_words = out_1[0].rearrange("p n t -> p (n t)").bitcast(I32)
-        for b, (v0, width) in enumerate(BLOCKS):
+        for b, (v0, pieces) in enumerate(BLOCKS):
+            width = sum(pieces)
             cols = slice(v0, v0 + width)
             s, c0 = divmod(v0, HALF)
             second = ring[:, b % 2 : b % 2 + PACK, :width]
@@ -214,22 +235,21 @@ def tile_picked_wdime_silu_lo_kernel(
                 second.rearrange("p t (c i) -> p c t i", i=2),
                 ADD,
             )
-            z_codes, z_scales = quantize("z%d" % b, z[:].rearrange("p c t -> p (c t)"), 1)
+            z_codes = sbuf("z_codes%d" % b, [P, width], U32)
+            z_scales = sbuf("z_scales%d" % b, [P, width], U8)
+            quantize_pieces(z_codes[:], z_scales[:], z, pieces)
             y_bf = sbuf("y_bf%d" % b, [P, width, PACK], BF16)
-            y = sbuf("y%d" % b, [P, PACK, width], F32)
             for u0 in range(0, width, BLOCK):
-                part = slice(u0, u0 + BLOCK)
+                n = min(BLOCK, width - u0)
+                part = slice(u0, u0 + n)
+                y = sbuf("y%d" % (v0 + u0), [P, PACK, n], F32)
                 bank = psum.tile([P, PACK, BLOCK], F32, name="out_bank", tag="acc_bank")
                 for t in range(PACK):
-                    matmul(bank[:, t, :], w2_q, t, z_codes[:, part], z_scales[:, part])
-                nc.scalar.activation(out=y_bf[:, part, :], in_=bank[:].rearrange("p t c -> p c t"), func=SILU)
-                nc.scalar.activation(out=y[:, :, part], in_=bank[:], func=SILU)
-            nc.vector.quantize_mx(
-                out=out_codes[:, cols].bitcast(FP8X4),
-                scales=out_scales[:, cols],
-                in_=y_bf[:].rearrange("p c t -> p (c t)"),
-            )
-            nc.sync.dma_start(out=out_rows[:, :, cols], in_=y[:])
+                    matmul(bank[:, t, :n], w2_q, t, z_codes[:, part], z_scales[:, part])
+                nc.scalar.activation(out=y_bf[:, part, :], in_=bank[:, :, :n].rearrange("p t c -> p c t"), func=SILU)
+                nc.scalar.activation(out=y[:], in_=bank[:, :, :n], func=SILU)
+                nc.sync.dma_start(out=out_rows[:, :, v0 + u0 : v0 + u0 + n], in_=y[:])
+            quantize_pieces(out_codes[:, cols], out_scales[:, cols], y_bf, pieces)
             nc.sync.dma_start(out=out_words[:, cols], in_=out_codes[:, cols].bitcast(I32))
 
         for q in range(QUADS):

@@ -1,6 +1,7 @@
 from contextlib import ExitStack
 
 import concourse.mybir as mybir
+from concourse.masks import make_identity
 
 K, T, H, J, U = 1024, 512, 512, 512, 1024
 FLOPS = 2 * (K * H * T + J * H * U + H * H * T)
@@ -35,7 +36,7 @@ def tile_picked_wdime_silu_lo_kernel(
 
     with ExitStack() as ctx:
         keep = ctx.enter_context(tc.tile_pool(name="keep", bufs=1))
-        psum = ctx.enter_context(tc.psum_pool(name="psum", bufs=4))
+        psum = ctx.enter_context(tc.psum_pool(name="psum", bufs=1))
 
         def sbuf(name, shape, dtype, tag=None):
             return keep.tile(shape, dtype, name=name, tag=tag or name, align_bytes=64)
@@ -68,7 +69,7 @@ def tile_picked_wdime_silu_lo_kernel(
             else:
                 nc.scalar.copy(out=out, in_=in_)
 
-        def quantize_weights(name, raw, engines):
+        def quantize_weights(name, raw, engines, calls=1):
             codes = sbuf(name + "_codes", [P, H], U32)
             scales = sbuf(name + "_scales", [P, H], U8)
             src = raw[:].rearrange("p j (m u e) -> p u m j e", u=2, e=2)
@@ -76,11 +77,8 @@ def tile_picked_wdime_silu_lo_kernel(
                 grouped = sbuf("%s_bf%d" % (name, u), [P, 2, P, PACK], BF16)
                 copy_on(engine, grouped[:].rearrange("p e m j -> p m j e"), src[:, u])
                 cols = slice(2 * P * u, 2 * P * (u + 1))
-                nc.vector.quantize_mx(
-                    out=codes[:, cols].bitcast(FP8X4),
-                    scales=scales[:, cols],
-                    in_=grouped[:].rearrange("p e m j -> p (e m j)"),
-                )
+                pieces = (P, P) if (calls == 2 and u == 0) else (2 * P,)
+                quantize_pieces(codes[:, cols], scales[:, cols], grouped[:].rearrange("p e m j -> p (e m) j"), pieces)
             return codes, scales
 
         def round_columns(name, raw, vector_cols):
@@ -135,6 +133,8 @@ def tile_picked_wdime_silu_lo_kernel(
 
         x_plane = sbuf("x_plane", [P, passes, T], U8)
         w2_plane_raw = sbuf("w2_plane_raw", [P, 1, H], U8)
+        identity = sbuf("identity", [P, P], F32)
+        make_identity(nc, identity[:])
         x_rows = sbuf("x_rows", [P, passes, T], U8)
         nc.vector.memset(x_plane[:].bitcast(I32), 0)
         nc.gpsimd.memset(w2_plane_raw[:].bitcast(I32), 0)
@@ -144,11 +144,11 @@ def tile_picked_wdime_silu_lo_kernel(
         a0_raw = load_rows("a0_raw", aT[:, :T])
         load_scales(nc.sync, x_rows, x_scales)
         w1_raw = [load_rows("w1_raw0", w1[:K_PASS, :])]
-        offsets = [load_list("offsets1", pos1)]
         w1_raw.append(load_rows("w1_raw1", w1[K_PASS:, :]))
-        offsets.append(load_list("offsets2", pos2))
         x_codes = [load_words("x_codes%d" % g, x_words[g]) for g in range(passes)]
+        offsets = [load_list("offsets1", pos1)]
         w2_raw = load_words("w2_raw", w2_words[0])
+        offsets.append(load_list("offsets2", pos2))
         a1_raw = [load_rows("a1_raw%d" % s, aT[:, T + HALF * s : T + HALF * (s + 1)]) for s in range(T // HALF)]
 
         w3_q = quantize_weights("w3", w3_raw, ("vector", "scalar"))
@@ -158,11 +158,11 @@ def tile_picked_wdime_silu_lo_kernel(
             nc.vector.tensor_copy(out=x_plane[rows].bitcast(I32), in_=x_rows[rows].bitcast(I32))
         w1_q = [
             quantize_weights("w1_0", w1_raw[0], ("vector", "vector")),
-            quantize_weights("w1_1", w1_raw[1], ("vector", "scalar")),
+            quantize_weights("w1_1", w1_raw[1], ("vector", "scalar"), 2),
         ]
         f0 = []
         for t in range(PACK):
-            bank = psum.tile([P, T], F32, name="f_bank", tag="f_bank")
+            bank = psum.tile([P, T], F32, name="f_bank", tag="f_bank", bufs=3)
             matmul(bank[:], w3_q, t, a0_codes[:], a0_scales[:])
             f0.append(sbuf("f0_%d" % t, [P, T], F32))
             nc.scalar.copy(out=f0[t][:], in_=bank[:])
@@ -176,7 +176,7 @@ def tile_picked_wdime_silu_lo_kernel(
 
         h = []
         for t in range(PACK):
-            bank = psum.tile([P, T], F32, name="h_bank", tag="acc_bank")
+            bank = psum.tile([P, T], F32, name="h_bank", tag="acc_bank", bufs=4)
             for g in range(passes):
                 matmul(bank[:], w1_q[g], t, x_codes[g][:], x_plane[:, g, :], start=(g == 0), stop=(g == passes - 1))
             h.append(sbuf("h_%d" % t, [P, T], F32))
@@ -194,7 +194,7 @@ def tile_picked_wdime_silu_lo_kernel(
             codes, scales = quantize("a1_%d" % s, round_columns("a1_bf%d" % s, a1_raw[s][:], 0), 1)
             pairs = []
             for u in range(PACK // 2):
-                bank = psum.tile([P, 2, HALF], F32, name="f_bank", tag="f_bank")
+                bank = psum.tile([P, 2, HALF], F32, name="f_bank", tag="f_bank", bufs=3)
                 for e in range(2):
                     matmul(bank[:, e, :], w3_q, 2 * u + e, codes[:], scales[:])
                 pairs.append(sbuf("f1_%d_%d" % (s, u), [P, 2, HALF], F32))
@@ -212,45 +212,96 @@ def tile_picked_wdime_silu_lo_kernel(
                 gather(tile[:, t, :], t, 0, v0, width, f0[t][:, v0 : v0 + width])
             first.append(tile)
 
-        ring = sbuf("ring", [P, PACK + 1, HALF], F32, tag="a1_bf1")
+        ring = sbuf("ring", [P, PACK + 1, BLOCK], F32)
         out_codes = sbuf("out_codes", [P, T], U32)
         out_scales = sbuf("out_scales", [P, T], U8)
         out_rows = out_0.rearrange("(p t) v -> p t v", t=PACK)
         out_words = out_1[0].rearrange("p n t -> p (n t)").bitcast(I32)
-        for b, (v0, pieces) in enumerate(BLOCKS):
+        def sum_on_tensor(addend, second, z):
+            width = z.shape[1]
+            banks = [psum.tile([P, PACK, P], F32, name="sum_bank", tag="acc_bank", bufs=4) for u0 in range(0, width, P)]
+            for t in range(PACK):
+                for n, bank in enumerate(banks):
+                    part = slice(P * n, P * (n + 1))
+                    for term, opens in ((addend, True), (second, False)):
+                        nc.tensor.matmul(
+                            bank[:, t, :], term[:, t, part], identity[:], is_transpose=True, start=opens, stop=not opens
+                        )
+            back = psum.tile([P, 2, width], F32, name="back_bank", tag="late_bank")
+            for n, bank in enumerate(banks):
+                turned = sbuf("turned%d" % n, [P, 2, P, 2], BF16)
+                nc.scalar.copy(out=turned[:], in_=bank[:].rearrange("v (u e) p -> v u p e", e=2))
+                words = turned[:].rearrange("v u p e -> v (u p e)").bitcast(F32)
+                for u in range(2):
+                    nc.tensor.transpose(back[:, u, P * n : P * (n + 1)], words[:, P * u : P * (u + 1)], identity[:])
+            nc.scalar.copy(
+                out=z[:].rearrange("p c t -> p (c t)").bitcast(F32).rearrange("p (c u) -> p c u", u=2),
+                in_=back[:].rearrange("p u c -> p c u"),
+            )
+
+        def sum_block(b):
+            v0, pieces = BLOCKS[b]
             width = sum(pieces)
             cols = slice(v0, v0 + width)
             s, c0 = divmod(v0, HALF)
-            second = ring[:, b % 2 : b % 2 + PACK, :width]
+            if b == 0:
+                whole = sbuf("second0", [P, PACK, width], F32, tag="a1_bf1")
+                second = whole[:]
+            else:
+                second = ring[:, b % 2 : b % 2 + PACK, :width]
             for t in range(PACK) if b % 2 == 0 else (PACK - 1, *range(PACK - 1)):
                 gather(second[:, t, :], t, 1, v0, width, f1[s][t // 2][:, t % 2, c0 : c0 + width])
             if v0 < FIRST_CUT:
                 addend = first[0][:, :, cols]
             else:
                 addend = first[1][:, :, v0 - FIRST_CUT : v0 - FIRST_CUT + width]
-            z = sbuf("z%d" % b, [P, width, PACK], BF16)
-            nc.vector.tensor_tensor(
-                z[:].rearrange("p (c i) t -> p c t i", i=2),
-                addend.rearrange("p t (c i) -> p c t i", i=2),
-                second.rearrange("p t (c i) -> p c t i", i=2),
-                ADD,
-            )
+            z = sbuf("z%d" % b, [P, width, PACK], BF16, tag="z0" if b == 2 else None)
+            if b == 0:
+                sum_on_tensor(addend, second, z)
+            else:
+                nc.vector.tensor_tensor(
+                    z[:].rearrange("p (c i) t -> p c t i", i=2),
+                    addend.rearrange("p t (c i) -> p c t i", i=2),
+                    second.rearrange("p t (c i) -> p c t i", i=2),
+                    ADD,
+                )
+            return z
+
+        def project_block(b, z):
+            v0, pieces = BLOCKS[b]
+            width = sum(pieces)
+            cols = slice(v0, v0 + width)
             z_codes = sbuf("z_codes%d" % b, [P, width], U32)
             z_scales = sbuf("z_scales%d" % b, [P, width], U8)
-            quantize_pieces(z_codes[:], z_scales[:], z, pieces)
+            quantize_pieces(z_codes[:], z_scales[:], z[:], pieces)
             y_bf = sbuf("y_bf%d" % b, [P, width, PACK], BF16)
+            y = sbuf("y%d" % b, [P, PACK, width], F32)
             for u0 in range(0, width, BLOCK):
-                n = min(BLOCK, width - u0)
-                part = slice(u0, u0 + n)
-                y = sbuf("y%d" % (v0 + u0), [P, PACK, n], F32)
-                bank = psum.tile([P, PACK, BLOCK], F32, name="out_bank", tag="acc_bank")
+                part = slice(u0, u0 + BLOCK)
+                if b == 1:
+                    bank = psum.tile([P, PACK, BLOCK], F32, name="out_bank", tag="late_bank")
+                else:
+                    bank = psum.tile([P, PACK, BLOCK], F32, name="out_bank", tag="acc_bank", bufs=4)
                 for t in range(PACK):
-                    matmul(bank[:, t, :n], w2_q, t, z_codes[:, part], z_scales[:, part])
-                nc.scalar.activation(out=y_bf[:, part, :], in_=bank[:, :, :n].rearrange("p t c -> p c t"), func=SILU)
-                nc.scalar.activation(out=y[:], in_=bank[:, :, :n], func=SILU)
-                nc.sync.dma_start(out=out_rows[:, :, v0 + u0 : v0 + u0 + n], in_=y[:])
-            quantize_pieces(out_codes[:, cols], out_scales[:, cols], y_bf, pieces)
-            nc.sync.dma_start(out=out_words[:, cols], in_=out_codes[:, cols].bitcast(I32))
+                    matmul(bank[:, t, :], w2_q, t, z_codes[:, part], z_scales[:, part])
+                if b == 2:
+                    nc.scalar.activation(out=y_bf[:, part, :], in_=bank[:].rearrange("p t c -> p c t"), func=SILU)
+                nc.scalar.activation(out=y[:, :, part], in_=bank[:], func=SILU)
+                if b != 2:
+                    nc.vector.tensor_copy(
+                        out=y_bf[:, part, :].rearrange("p (c i) t -> p c t i", i=2),
+                        in_=y[:, :, part].rearrange("p t (c i) -> p c t i", i=2),
+                    )
+            nc.sync.dma_start(out=out_rows[:, :, cols], in_=y[:])
+            quantize_pieces(out_codes[:, cols], out_scales[:, cols], y_bf[:], (BLOCK,) * (width // BLOCK))
+            if b != 1:
+                done = slice(0, FIRST_CUT) if b == 0 else cols
+                nc.sync.dma_start(out=out_words[:, done], in_=out_codes[:, done].bitcast(I32))
+
+        z_first = sum_block(0)
+        project_block(1, sum_block(1))
+        project_block(0, z_first)
+        project_block(2, sum_block(2))
 
         for q in range(QUADS):
             queue = nc.sync if q < 2 else nc.scalar

from contextlib import ExitStack

import concourse.mybir as mybir
from concourse.masks import make_identity

K, T, H, J, U = 1024, 512, 512, 512, 1024
FLOPS = 2 * (K * H * T + J * H * U + H * H * T)

F32 = mybir.dt.float32
BF16 = mybir.dt.bfloat16
I32 = mybir.dt.int32
U32 = mybir.dt.uint32
U16 = mybir.dt.uint16
U8 = mybir.dt.uint8
FP8X4 = mybir.dt.float8_e4m3fn_x4
SILU = mybir.ActivationFunctionType.Silu
MULT = mybir.AluOpType.mult
ADD = mybir.AluOpType.add

P = 128
PACK = 4
K_PASS = P * PACK
QUADS = 4
HALF = 256
BLOCK = 128
VECTOR_COLS = 352
FIRST_CUT = 384
BLOCKS = ((0, (256,)), (256, (128,)), (384, (128,)))


def tile_picked_wdime_silu_lo_kernel(
    tc, x_words, x_scales, aT, w1, w3, w2_words, w2_scales, pos1, pos2, out_0, out_1, out_2
):
    nc = tc.nc
    passes = K // K_PASS

    with ExitStack() as ctx:
        keep = ctx.enter_context(tc.tile_pool(name="keep", bufs=1))
        psum = ctx.enter_context(tc.psum_pool(name="psum", bufs=1))

        def sbuf(name, shape, dtype, tag=None):
            return keep.tile(shape, dtype, name=name, tag=tag or name, align_bytes=64)

        def load_rows(name, rows):
            raw = sbuf(name, [P, PACK, rows.shape[1]], F32)
            nc.sync.dma_start(out=raw[:], in_=rows.rearrange("(p j) c -> p j c", j=PACK))
            return raw

        def load_words(name, words):
            tile = sbuf(name, [P, words.shape[1]], U32)
            nc.sync.dma_start(out=tile[:].bitcast(I32), in_=words.rearrange("p n t -> p (n t)").bitcast(I32))
            return tile

        def load_scales(queue, plane, scales):
            for q in range(QUADS):
                queue.dma_start(
                    out=plane[32 * q : 32 * q + 4].bitcast(I32),
                    in_=scales[:, 4 * q : 4 * q + 4, :].rearrange("g r c -> r g c").bitcast(I32),
                )

        def load_list(name, pos):
            offsets = keep.tile([P, T // 16], U16, name=name)
            nc.sync.dma_start(offsets[:], pos)
            return offsets

        def copy_on(engine, out, in_):
            if engine == "vector":
                nc.vector.tensor_copy(out=out, in_=in_)
            else:
                nc.scalar.copy(out=out, in_=in_)

        def quantize_weights(name, raw, engines, calls=1):
            codes = sbuf(name + "_codes", [P, H], U32)
            scales = sbuf(name + "_scales", [P, H], U8)
            src = raw[:].rearrange("p j (m u e) -> p u m j e", u=2, e=2)
            for u, engine in enumerate(engines):
                grouped = sbuf("%s_bf%d" % (name, u), [P, 2, P, PACK], BF16)
                copy_on(engine, grouped[:].rearrange("p e m j -> p m j e"), src[:, u])
                cols = slice(2 * P * u, 2 * P * (u + 1))
                pieces = (P, P) if (calls == 2 and u == 0) else (2 * P,)
                quantize_pieces(codes[:, cols], scales[:, cols], grouped[:].rearrange("p e m j -> p (e m) j"), pieces)
            return codes, scales

        def round_columns(name, raw, vector_cols):
            width = raw.shape[2]
            grouped = sbuf(name, [P, width, PACK], BF16)
            dst = grouped[:].rearrange("p (c i) j -> p c j i", i=2)
            src = raw.rearrange("p j (c i) -> p c j i", i=2)
            cut = vector_cols // 2
            if cut:
                copy_on("vector", dst[:, :cut], src[:, :cut])
            copy_on("scalar", dst[:, cut:], src[:, cut:])
            return grouped[:].rearrange("p c j -> p (c j)")

        def quantize(name, grouped, calls):
            width = grouped.shape[1] // PACK
            codes = sbuf(name + "_codes", [P, width], U32)
            scales = sbuf(name + "_scales", [P, width], U8)
            step = width // calls
            for c0 in range(0, width, step):
                nc.vector.quantize_mx(
                    out=codes[:, c0 : c0 + step].bitcast(FP8X4),
                    scales=scales[:, c0 : c0 + step],
                    in_=grouped[:, PACK * c0 : PACK * (c0 + step)],
                )
            return codes, scales

        def quantize_pieces(codes, scales, grouped, pieces):
            c0 = 0
            for n in pieces:
                nc.vector.quantize_mx(
                    out=codes[:, c0 : c0 + n].bitcast(FP8X4),
                    scales=scales[:, c0 : c0 + n],
                    in_=grouped[:, c0 : c0 + n, :].rearrange("p c t -> p (c t)"),
                )
                c0 += n

        def matmul(out, weights, t, codes, scales, start=True, stop=True):
            cols = slice(P * t, P * (t + 1))
            nc.tensor.matmul_mx(
                out=out,
                lhsT=weights[0][:, cols].bitcast(FP8X4),
                lhsT_scale=weights[1][:, cols],
                rhs=codes.bitcast(FP8X4),
                rhs_scale=scales,
                start=start,
                stop=stop,
            )

        warm = sbuf("warm", [P, 2], F32)
        nc.vector.memset(warm[:, 0:1], 0.0)
        nc.scalar.activation(out=warm[:, 1:2], in_=warm[:, 0:1], func=SILU)

        x_plane = sbuf("x_plane", [P, passes, T], U8)
        w2_plane_raw = sbuf("w2_plane_raw", [P, 1, H], U8)
        identity = sbuf("identity", [P, P], F32)
        make_identity(nc, identity[:])
        x_rows = sbuf("x_rows", [P, passes, T], U8)
        nc.vector.memset(x_plane[:].bitcast(I32), 0)
        nc.gpsimd.memset(w2_plane_raw[:].bitcast(I32), 0)
        load_scales(nc.gpsimd, w2_plane_raw, w2_scales)

        w3_raw = load_rows("w3_raw", w3)
        a0_raw = load_rows("a0_raw", aT[:, :T])
        load_scales(nc.sync, x_rows, x_scales)
        w1_raw = [load_rows("w1_raw0", w1[:K_PASS, :])]
        w1_raw.append(load_rows("w1_raw1", w1[K_PASS:, :]))
        x_codes = [load_words("x_codes%d" % g, x_words[g]) for g in range(passes)]
        offsets = [load_list("offsets1", pos1)]
        w2_raw = load_words("w2_raw", w2_words[0])
        offsets.append(load_list("offsets2", pos2))
        a1_raw = [load_rows("a1_raw%d" % s, aT[:, T + HALF * s : T + HALF * (s + 1)]) for s in range(T // HALF)]

        w3_q = quantize_weights("w3", w3_raw, ("vector", "scalar"))
        a0_codes, a0_scales = quantize("a0", round_columns("a0_bf", a0_raw[:], VECTOR_COLS), 1)
        for q in range(QUADS):
            rows = slice(32 * q, 32 * q + 4)
            nc.vector.tensor_copy(out=x_plane[rows].bitcast(I32), in_=x_rows[rows].bitcast(I32))
        w1_q = [
            quantize_weights("w1_0", w1_raw[0], ("vector", "vector")),
            quantize_weights("w1_1", w1_raw[1], ("vector", "scalar"), 2),
        ]
        f0 = []
        for t in range(PACK):
            bank = psum.tile([P, T], F32, name="f_bank", tag="f_bank", bufs=3)
            matmul(bank[:], w3_q, t, a0_codes[:], a0_scales[:])
            f0.append(sbuf("f0_%d" % t, [P, T], F32))
            nc.scalar.copy(out=f0[t][:], in_=bank[:])


        w2_plane = sbuf("w2_plane", [P, H], U8, tag="w1_1_bf0")
        nc.vector.tensor_copy(
            out=w2_plane[:].rearrange("p (t m) -> p m t", t=PACK),
            in_=w2_plane_raw[:, 0, :].rearrange("p (m t) -> p m t", t=PACK),
        )

        h = []
        for t in range(PACK):
            bank = psum.tile([P, T], F32, name="h_bank", tag="acc_bank", bufs=4)
            for g in range(passes):
                matmul(bank[:], w1_q[g], t, x_codes[g][:], x_plane[:, g, :], start=(g == 0), stop=(g == passes - 1))
            h.append(sbuf("h_%d" % t, [P, T], F32))
            nc.scalar.activation(out=h[t][:], in_=bank[:], func=SILU)

        w2_codes = sbuf("w2_codes", [P, H], U32, tag="w1_1_bf1")
        nc.vector.tensor_copy(
            out=w2_codes[:].bitcast(I32).rearrange("p (t m) -> p m t", t=PACK),
            in_=w2_raw[:].bitcast(I32).rearrange("p (m t) -> p m t", t=PACK),
        )
        w2_q = (w2_codes, w2_plane)

        f1 = []
        for s in range(T // HALF):
            codes, scales = quantize("a1_%d" % s, round_columns("a1_bf%d" % s, a1_raw[s][:], 0), 1)
            pairs = []
            for u in range(PACK // 2):
                bank = psum.tile([P, 2, HALF], F32, name="f_bank", tag="f_bank", bufs=3)
                for e in range(2):
                    matmul(bank[:, e, :], w3_q, 2 * u + e, codes[:], scales[:])
                pairs.append(sbuf("f1_%d_%d" % (s, u), [P, 2, HALF], F32))
                nc.scalar.copy(out=pairs[u][:], in_=bank[:])
            f1.append(pairs)

        def gather(out, t, d, v0, width, factor):
            picks = offsets[d][:, v0 // 16 : (v0 + width) // 16]
            nc.vector.tensor_tensor(out, h[t][:].indirect(picks), factor, MULT)

        first = []
        for v0, width, tag in ((0, FIRST_CUT, None), (FIRST_CUT, T - FIRST_CUT, "a1_bf0")):
            tile = sbuf("first%d" % v0, [P, PACK, width], F32, tag=tag)
            for t in range(PACK):
                gather(tile[:, t, :], t, 0, v0, width, f0[t][:, v0 : v0 + width])
            first.append(tile)

        ring = sbuf("ring", [P, PACK + 1, BLOCK], F32)
        out_codes = sbuf("out_codes", [P, T], U32)
        out_scales = sbuf("out_scales", [P, T], U8)
        out_rows = out_0.rearrange("(p t) v -> p t v", t=PACK)
        out_words = out_1[0].rearrange("p n t -> p (n t)").bitcast(I32)
        def sum_on_tensor(addend, second, z):
            width = z.shape[1]
            banks = [psum.tile([P, PACK, P], F32, name="sum_bank", tag="acc_bank", bufs=4) for u0 in range(0, width, P)]
            for t in range(PACK):
                for n, bank in enumerate(banks):
                    part = slice(P * n, P * (n + 1))
                    for term, opens in ((addend, True), (second, False)):
                        nc.tensor.matmul(
                            bank[:, t, :], term[:, t, part], identity[:], is_transpose=True, start=opens, stop=not opens
                        )
            back = psum.tile([P, 2, width], F32, name="back_bank", tag="late_bank")
            for n, bank in enumerate(banks):
                turned = sbuf("turned%d" % n, [P, 2, P, 2], BF16)
                nc.scalar.copy(out=turned[:], in_=bank[:].rearrange("v (u e) p -> v u p e", e=2))
                words = turned[:].rearrange("v u p e -> v (u p e)").bitcast(F32)
                for u in range(2):
                    nc.tensor.transpose(back[:, u, P * n : P * (n + 1)], words[:, P * u : P * (u + 1)], identity[:])
            nc.scalar.copy(
                out=z[:].rearrange("p c t -> p (c t)").bitcast(F32).rearrange("p (c u) -> p c u", u=2),
                in_=back[:].rearrange("p u c -> p c u"),
            )

        def sum_block(b):
            v0, pieces = BLOCKS[b]
            width = sum(pieces)
            cols = slice(v0, v0 + width)
            s, c0 = divmod(v0, HALF)
            if b == 0:
                whole = sbuf("second0", [P, PACK, width], F32, tag="a1_bf1")
                second = whole[:]
            else:
                second = ring[:, b % 2 : b % 2 + PACK, :width]
            for t in range(PACK) if b % 2 == 0 else (PACK - 1, *range(PACK - 1)):
                gather(second[:, t, :], t, 1, v0, width, f1[s][t // 2][:, t % 2, c0 : c0 + width])
            if v0 < FIRST_CUT:
                addend = first[0][:, :, cols]
            else:
                addend = first[1][:, :, v0 - FIRST_CUT : v0 - FIRST_CUT + width]
            z = sbuf("z%d" % b, [P, width, PACK], BF16, tag="z0" if b == 2 else None)
            if b == 0:
                sum_on_tensor(addend, second, z)
            else:
                nc.vector.tensor_tensor(
                    z[:].rearrange("p (c i) t -> p c t i", i=2),
                    addend.rearrange("p t (c i) -> p c t i", i=2),
                    second.rearrange("p t (c i) -> p c t i", i=2),
                    ADD,
                )
            return z

        def project_block(b, z):
            v0, pieces = BLOCKS[b]
            width = sum(pieces)
            cols = slice(v0, v0 + width)
            z_codes = sbuf("z_codes%d" % b, [P, width], U32)
            z_scales = sbuf("z_scales%d" % b, [P, width], U8)
            quantize_pieces(z_codes[:], z_scales[:], z[:], pieces)
            y_bf = sbuf("y_bf%d" % b, [P, width, PACK], BF16)
            y = sbuf("y%d" % b, [P, PACK, width], F32)
            for u0 in range(0, width, BLOCK):
                part = slice(u0, u0 + BLOCK)
                if b == 1:
                    bank = psum.tile([P, PACK, BLOCK], F32, name="out_bank", tag="late_bank")
                else:
                    bank = psum.tile([P, PACK, BLOCK], F32, name="out_bank", tag="acc_bank", bufs=4)
                for t in range(PACK):
                    matmul(bank[:, t, :], w2_q, t, z_codes[:, part], z_scales[:, part])
                if b == 2:
                    nc.scalar.activation(out=y_bf[:, part, :], in_=bank[:].rearrange("p t c -> p c t"), func=SILU)
                nc.scalar.activation(out=y[:, :, part], in_=bank[:], func=SILU)
                if b != 2:
                    nc.vector.tensor_copy(
                        out=y_bf[:, part, :].rearrange("p (c i) t -> p c t i", i=2),
                        in_=y[:, :, part].rearrange("p t (c i) -> p c t i", i=2),
                    )
            nc.sync.dma_start(out=out_rows[:, :, cols], in_=y[:])
            quantize_pieces(out_codes[:, cols], out_scales[:, cols], y_bf[:], (BLOCK,) * (width // BLOCK))
            if b != 1:
                done = slice(0, FIRST_CUT) if b == 0 else cols
                nc.sync.dma_start(out=out_words[:, done], in_=out_codes[:, done].bitcast(I32))

        z_first = sum_block(0)
        project_block(1, sum_block(1))
        project_block(0, z_first)
        project_block(2, sum_block(2))

        for q in range(QUADS):
            queue = nc.sync if q < 2 else nc.scalar
            queue.dma_start(
                out=out_2[0][4 * q : 4 * q + 4, :].bitcast(I32),
                in_=out_scales[32 * q : 32 * q + 4, :].bitcast(I32),
            )
